import numpy as np
import ml_dtypes


def mxq(x, axis, fmt="e4m3"):
    dtype, down = {"e4m3": (ml_dtypes.float8_e4m3fn, 7), "e5m2": (ml_dtypes.float8_e5m2, 14)}[fmt]
    v = np.moveaxis(np.asarray(x, np.float32).astype(ml_dtypes.bfloat16).astype(np.float64), axis, -1)
    blocks = v.reshape(v.shape[:-1] + (-1, 32))
    amax = np.abs(blocks).max(-1, keepdims=True)
    byte = np.maximum(np.where(amax > 0, np.frexp(amax)[1] - 1 + 127, 0) - down, 1)
    scale = np.exp2(byte - 127.0)
    codes = (blocks / scale).astype(np.float32).astype(dtype).astype(np.float64)
    return np.moveaxis((codes * scale).reshape(v.shape), -1, axis)


WIDE = False


def mx_kscale(k):
    if not WIDE:
        return np.ones(k)
    levels = np.array([10, -10, 5, -5, 0])
    if k % 512:
        return np.exp2(np.random.permutation(np.resize(levels, k // 32))).repeat(32)
    a = np.empty((k // 512, 16))
    for p in range(k // 512):
        a[p, :8] = np.random.permutation(np.resize(levels, 8))
        for g in range(8):
            far = levels[np.abs(levels - a[p, g]) >= 10]
            a[p, g + 8] = far[np.random.randint(len(far))]
    return np.exp2(a.ravel()).repeat(32)


def f64(x):
    return np.asarray(x).astype(np.float64)


def striped(idx):
    return np.tile(idx.reshape(-1, 16).T, (8, 1)).astype(np.uint16)


def unstriped(offs):
    return offs[:16].T.reshape(-1).astype(np.int64)


E2M1 = np.array([0.0, 0.5, 1.0, 1.5, 2.0, 3.0, 4.0, 6.0, -0.0, -0.5, -1.0, -1.5, -2.0, -3.0, -4.0, -6.0])


def pack_fp4(w):
    k, n = w.shape
    w = f64(np.asarray(w, np.float32).astype(ml_dtypes.bfloat16)).reshape(k // 32, 32, n)
    amax = np.abs(w).max(1)
    mant, ex = np.frexp(amax / 6.0)
    byte = np.clip(np.where(amax > 0, np.where(mant > 0.5, ex, ex - 1) + 127, 1), 1, 254)
    scaled = (w * np.exp2(127.0 - byte)[:, None, :]).reshape(k, n).astype(np.float32)
    c = np.ascontiguousarray(scaled.reshape(k // 512, 128, 4, n).transpose(0, 1, 3, 2)).astype(ml_dtypes.float4_e2m1fn).view(np.uint8) & 0xF
    words = (c[..., 0::2] | (c[..., 1::2] << 4)).reshape(k // 512, 128, 2 * n)
    return np.ascontiguousarray(words), np.ascontiguousarray(byte.astype(np.uint8).reshape(k // 512, 16, n))


def unpack_fp4(words, scales):
    g, _, n = scales.shape
    words = np.ascontiguousarray(words).reshape(g, 128, n, 2)
    nib = np.empty((g, 128, n, 4), np.uint8)
    nib[..., 0::2] = words & 0xF
    nib[..., 1::2] = words >> 4
    vals = E2M1[nib] * np.repeat(np.exp2(scales.astype(np.float64) - 127.0), 8, axis=1)[..., None]
    return vals.transpose(0, 1, 3, 2).reshape(g * 512, n)


K, T, S, V, N = 512, 2048, 1024, 512, 128
P = 2 ** 7


def setup_inputs():
    n = np.random.standard_normal
    s = mx_kscale(K)[:, None]
    packed_w1 = pack_fp4(n((K, N)) / np.sqrt(K) / s)
    return {
        "xT": (n((K, T)) * s).astype(np.float32),
        "w1_words": packed_w1[0],
        "w1_scales": packed_w1[1],
        "frac": np.tile(np.random.uniform(0.05, 0.95, V), (P, 1)).astype(np.float32),
        "offs": striped(np.random.permutation(T)[:S]),
        "left": striped(np.random.permutation(S)[:V]),
        "right": striped(np.random.permutation(S)[:V]),
    }


def reference(xT, w1_words, w1_scales, frac, offs, left, right):
    xq = mxq(f64(xT)[:, unstriped(offs)], 0, "e4m3")
    y = unpack_fp4(w1_words, w1_scales).T @ xq
    l = y[:, unstriped(left)]
    return l + (y[:, unstriped(right)] - l) * f64(frac)[:1]

@@ -1,0 +1,126 @@
+from contextlib import ExitStack
+
+import concourse.mybir as mybir
+
+K, T, S, V, N = 512, 2048, 1024, 512, 128
+P = 128
+FLOPS = 2 * K * N * S
+
+F32 = mybir.dt.float32
+BF16 = mybir.dt.bfloat16
+I32 = mybir.dt.int32
+U32 = mybir.dt.uint32
+U16 = mybir.dt.uint16
+U8 = mybir.dt.uint8
+FP8X4 = mybir.dt.float8_e4m3fn_x4
+FP4X4 = mybir.dt.float4_e2m1fn_x4
+MULT = mybir.AluOpType.mult
+ADD = mybir.AluOpType.add
+
+LOADS = (
+    ((1024, 1024), (1024, 640)),
+    ((1024, 256), (512, 512), (256, 256), (256, 256)),
+)
+PIECE = 256
+SAMPLES = (256, 256)
+
+
+def tile_picked_lerp_none_e_kernel(
+    tc, xT, w1_words, w1_scales, frac, offs, left, right, out
+):
+    nc = tc.nc
+    with ExitStack() as ctx:
+        keep = ctx.enter_context(tc.tile_pool(name="keep", bufs=1))
+        psum = ctx.enter_context(tc.psum_pool(name="psum", bufs=1))
+
+        offs_sb = keep.tile([P, S // 16], U16, name="offs_sb")
+        left_sb = keep.tile([P, V // 16], U16, name="left_sb")
+        right_sb = keep.tile([P, V // 16], U16, name="right_sb")
+        w_codes = keep.tile([P, 2 * N], U8, name="w_codes", align_bytes=64)
+        w_scales = keep.tile([P, N], U8, name="w_scales", align_bytes=64)
+        frac_sb = keep.tile([P, V], F32, name="frac_sb")
+        nc.gpsimd.memset(w_scales[:].bitcast(I32), 0)
+
+        x_rows = xT.rearrange("(p u e) t -> p u e t", u=2, e=2)
+        pairs = [keep.tile([P, 2 * T], BF16, name="pairs%d" % u, align_bytes=64) for u in range(2)]
+        picked = keep.tile([P, 2, S], U32, name="picked")
+
+        raw = {}
+        for u in range(2):
+            t0 = 0
+            for width, on_vector in LOADS[u]:
+                raw[u, t0] = keep.tile([P, 2, width], F32, name="raw%d_%d" % (u, t0))
+                nc.sync.dma_start(raw[u, t0][:], x_rows[:, u, :, t0 : t0 + width])
+                t0 = t0 + width
+            if u == 0:
+                nc.sync.dma_start(offs_sb[:], offs)
+        nc.sync.dma_start(w_codes[:].bitcast(I32), w1_words[0].bitcast(I32))
+        for q in range(4):
+            nc.sync.dma_start(
+                w_scales[32 * q : 32 * q + 4, :].bitcast(I32),
+                w1_scales[0, 4 * q : 4 * q + 4, :].bitcast(I32),
+            )
+        nc.sync.dma_start(right_sb[:], right)
+        nc.sync.dma_start(left_sb[:], left)
+        nc.sync.dma_start(frac_sb[:], frac)
+
+        def round_pairs(u):
+            t0 = 0
+            for width, on_vector in LOADS[u]:
+                woven = pairs[u][:, 2 * t0 : 2 * (t0 + width)].rearrange("p (t e) -> p t e", e=2)
+                source = raw[u, t0][:].rearrange("p e t -> p t e")
+                nc.vector.tensor_copy(woven[:, :on_vector, :], source[:, :on_vector, :])
+                if on_vector < width:
+                    nc.scalar.copy(woven[:, on_vector:, :], source[:, on_vector:, :])
+                t0 = t0 + width
+
+        round_pairs(0)
+        nc.vector.tensor_copy(picked[:, 0, :], pairs[0][:].bitcast(U32).indirect(offs_sb[:]))
+        round_pairs(1)
+
+        y = keep.tile([P, S], F32, name="y")
+        pieces = S // PIECE
+        for i in range(pieces):
+            cols = slice(i * PIECE, (i + 1) * PIECE)
+            entries = offs_sb[:, i * PIECE // 16 : (i + 1) * PIECE // 16]
+            nc.vector.tensor_copy(picked[:, 1, cols], pairs[1][:].bitcast(U32).indirect(entries))
+        for i in range(pieces):
+            cols = slice(i * PIECE, (i + 1) * PIECE)
+            grouped = keep.tile([P, 4 * PIECE], BF16, name="grouped%d" % i, tag="grouped%d" % i, align_bytes=64)
+            nc.scalar.copy(
+                grouped[:].bitcast(U32).rearrange("p (c u) -> p c u", u=2),
+                picked[:, :, cols].rearrange("p u c -> p c u"),
+            )
+            codes = keep.tile([P, PIECE], U32, name="codes%d" % i, align_bytes=64)
+            scales = keep.tile([P, PIECE], U8, name="scales%d" % i, align_bytes=64)
+            nc.vector.quantize_mx(out=codes[:].bitcast(FP8X4), scales=scales[:], in_=grouped[:])
+            acc = psum.tile([P, PIECE], F32, name="acc%d" % i)
+            nc.tensor.matmul_mx(
+                out=acc[:],
+                lhsT=w_codes[:].bitcast(FP4X4),
+                lhsT_scale=w_scales[:],
+                rhs=codes[:].bitcast(FP8X4),
+                rhs_scale=scales[:],
+                start=True,
+                stop=True,
+            )
+            if i == pieces - 2:
+                nc.vector.tensor_copy(y[:, cols], acc[:])
+            else:
+                nc.scalar.copy(y[:, cols], acc[:])
+
+        rest = keep.tile([P, V], F32, name="rest", tag="grouped%d" % (pieces - 1), align_bytes=64)
+        nc.vector.tensor_scalar(rest[:], frac_sb[:], -1.0, 1.0, MULT, ADD)
+
+        v0 = 0
+        for width in SAMPLES:
+            cols = slice(v0, v0 + width)
+            entries = slice(v0 // 16, (v0 + width) // 16)
+            from_right = keep.tile([P, width], F32, name="from_right%d" % v0)
+            from_left = keep.tile([P, width], F32, name="from_left%d" % v0)
+            result = keep.tile([P, width], F32, name="result%d" % v0)
+            nc.vector.tensor_tensor(from_right[:], y[:].indirect(right_sb[:, entries]), frac_sb[:, cols], MULT)
+            nc.vector.tensor_tensor(from_left[:], y[:].indirect(left_sb[:, entries]), rest[:, cols], MULT)
+            nc.vector.tensor_tensor(result[:], from_right[:], from_left[:], ADD)
+            nc.sync.dma_start(out[:, cols], result[:])
+            v0 = v0 + width

@@ -18,11 +18,11 @@ MULT = mybir.AluOpType.mult
 ADD = mybir.AluOpType.add
 
 LOADS = (
-    ((1024, 1024), (1024, 640)),
-    ((1024, 256), (512, 512), (256, 256), (256, 256)),
+    ((1024, 672), (1024, 672)),
+    ((1024, 384), (512, 336), (256, 128), (256, 256)),
 )
+SPLIT = T // 2
 PIECE = 256
-SAMPLES = (256, 256)
 
 
 def tile_picked_lerp_none_e_kernel(
@@ -42,24 +42,27 @@ def tile_picked_lerp_none_e_kernel(
         nc.gpsimd.memset(w_scales[:].bitcast(I32), 0)
 
         x_rows = xT.rearrange("(p u e) t -> p u e t", u=2, e=2)
+        raw = [keep.tile([P, 2, T], F32, name="raw%d" % u) for u in range(2)]
         pairs = [keep.tile([P, 2 * T], BF16, name="pairs%d" % u, align_bytes=64) for u in range(2)]
         picked = keep.tile([P, 2, S], U32, name="picked")
 
-        raw = {}
-        for u in range(2):
-            t0 = 0
-            for width, on_vector in LOADS[u]:
-                raw[u, t0] = keep.tile([P, 2, width], F32, name="raw%d_%d" % (u, t0))
-                nc.sync.dma_start(raw[u, t0][:], x_rows[:, u, :, t0 : t0 + width])
-                t0 = t0 + width
-            if u == 0:
-                nc.sync.dma_start(offs_sb[:], offs)
-        nc.sync.dma_start(w_codes[:].bitcast(I32), w1_words[0].bitcast(I32))
+        t0 = 0
+        for width, on_vector in LOADS[0]:
+            nc.sync.dma_start(raw[0][:, :, t0 : t0 + width], x_rows[:, 0, :, t0 : t0 + width])
+            t0 = t0 + width
+        nc.sync.dma_start(offs_sb[:], offs)
+        nc.sync.dma_start(raw[1][:, :, :SPLIT], x_rows[:, 1, :, :SPLIT])
+        nc.sync.dma_start(raw[1][:, 0, SPLIT:], x_rows[:, 1, 0, SPLIT:])
+        t0 = SPLIT
+        for width, on_vector in LOADS[1][1:]:
+            nc.sync.dma_start(raw[1][:, 1, t0 : t0 + width], x_rows[:, 1, 1, t0 : t0 + width])
+            t0 = t0 + width
         for q in range(4):
             nc.sync.dma_start(
                 w_scales[32 * q : 32 * q + 4, :].bitcast(I32),
                 w1_scales[0, 4 * q : 4 * q + 4, :].bitcast(I32),
             )
+        nc.sync.dma_start(w_codes[:].bitcast(I32), w1_words[0].bitcast(I32))
         nc.sync.dma_start(right_sb[:], right)
         nc.sync.dma_start(left_sb[:], left)
         nc.sync.dma_start(frac_sb[:], frac)
@@ -68,7 +71,7 @@ def tile_picked_lerp_none_e_kernel(
             t0 = 0
             for width, on_vector in LOADS[u]:
                 woven = pairs[u][:, 2 * t0 : 2 * (t0 + width)].rearrange("p (t e) -> p t e", e=2)
-                source = raw[u, t0][:].rearrange("p e t -> p t e")
+                source = raw[u][:, :, t0 : t0 + width].rearrange("p e t -> p t e")
                 nc.vector.tensor_copy(woven[:, :on_vector, :], source[:, :on_vector, :])
                 if on_vector < width:
                     nc.scalar.copy(woven[:, on_vector:, :], source[:, on_vector:, :])
@@ -94,33 +97,36 @@ def tile_picked_lerp_none_e_kernel(
             codes = keep.tile([P, PIECE], U32, name="codes%d" % i, align_bytes=64)
             scales = keep.tile([P, PIECE], U8, name="scales%d" % i, align_bytes=64)
             nc.vector.quantize_mx(out=codes[:].bitcast(FP8X4), scales=scales[:], in_=grouped[:])
-            acc = psum.tile([P, PIECE], F32, name="acc%d" % i)
-            nc.tensor.matmul_mx(
-                out=acc[:],
-                lhsT=w_codes[:].bitcast(FP4X4),
-                lhsT_scale=w_scales[:],
-                rhs=codes[:].bitcast(FP8X4),
-                rhs_scale=scales[:],
-                start=True,
-                stop=True,
-            )
-            if i == pieces - 2:
-                nc.vector.tensor_copy(y[:, cols], acc[:])
-            else:
-                nc.scalar.copy(y[:, cols], acc[:])
+            parts = 2 if i == pieces - 1 else 1
+            width = PIECE // parts
+            for h in range(parts):
+                part = slice(h * width, (h + 1) * width)
+                acc = psum.tile([P, width], F32, name="acc%d_%d" % (i, h))
+                nc.tensor.matmul_mx(
+                    out=acc[:],
+                    lhsT=w_codes[:].bitcast(FP4X4),
+                    lhsT_scale=w_scales[:],
+                    rhs=codes[:, part].bitcast(FP8X4),
+                    rhs_scale=scales[:, part],
+                    start=True,
+                    stop=True,
+                )
+                y_part = y[:, i * PIECE + h * width : i * PIECE + (h + 1) * width]
+                if h + 1 < parts:
+                    rest = keep.tile([P, V], F32, name="rest", tag="grouped%d" % i, align_bytes=64)
+                    nc.vector.tensor_scalar(rest[:], frac_sb[:], -1.0, 1.0, MULT, ADD)
+                    nc.vector.tensor_copy(y_part, acc[:])
+                else:
+                    nc.scalar.copy(y_part, acc[:])
 
-        rest = keep.tile([P, V], F32, name="rest", tag="grouped%d" % (pieces - 1), align_bytes=64)
-        nc.vector.tensor_scalar(rest[:], frac_sb[:], -1.0, 1.0, MULT, ADD)
-
-        v0 = 0
-        for width in SAMPLES:
-            cols = slice(v0, v0 + width)
-            entries = slice(v0 // 16, (v0 + width) // 16)
-            from_right = keep.tile([P, width], F32, name="from_right%d" % v0)
-            from_left = keep.tile([P, width], F32, name="from_left%d" % v0)
-            result = keep.tile([P, width], F32, name="result%d" % v0)
-            nc.vector.tensor_tensor(from_right[:], y[:].indirect(right_sb[:, entries]), frac_sb[:, cols], MULT)
-            nc.vector.tensor_tensor(from_left[:], y[:].indirect(left_sb[:, entries]), rest[:, cols], MULT)
-            nc.vector.tensor_tensor(result[:], from_right[:], from_left[:], ADD)
+        from_right = keep.tile([P, V], F32, name="from_right")
+        from_left = keep.tile([P, V], F32, name="from_left")
+        nc.vector.tensor_tensor(from_right[:], y[:].indirect(right_sb[:]), frac_sb[:], MULT)
+        halves = [slice(0, V // 2), slice(V // 2, V)]
+        for cols in halves:
+            entries = left_sb[:, cols.start // 16 : cols.stop // 16]
+            nc.vector.tensor_tensor(from_left[:, cols], y[:].indirect(entries), rest[:, cols], MULT)
+        for cols in halves:
+            result = keep.tile([P, V // 2], F32, name="result%d" % cols.start)
+            nc.vector.tensor_tensor(result[:], from_right[:, cols], from_left[:, cols], ADD)
             nc.sync.dma_start(out[:, cols], result[:])
-            v0 = v0 + width

@@ -16,12 +16,11 @@ FP8X4 = mybir.dt.float8_e4m3fn_x4
 FP4X4 = mybir.dt.float4_e2m1fn_x4
 MULT = mybir.AluOpType.mult
 ADD = mybir.AluOpType.add
+COPY = mybir.ActivationFunctionType.Copy
 
-LOADS = (
-    ((1024, 672), (1024, 672)),
-    ((1024, 384), (512, 336), (256, 128), (256, 256)),
-)
-SPLIT = T // 2
+PAIR_LOADS = ((1024, 384), (512, 336), (256, 176), (256, 176))
+ROW3_LOADS = (512, 512, 512, 512)
+ON_VECTOR = 2
 PIECE = 256
 
 
@@ -39,23 +38,25 @@ def tile_picked_lerp_none_e_kernel(
         w_codes = keep.tile([P, 2 * N], U8, name="w_codes", align_bytes=64)
         w_scales = keep.tile([P, N], U8, name="w_scales", align_bytes=64)
         frac_sb = keep.tile([P, V], F32, name="frac_sb")
-        nc.gpsimd.memset(w_scales[:].bitcast(I32), 0)
+        nc.vector.memset(w_scales[:].bitcast(I32), 0)
 
-        x_rows = xT.rearrange("(p u e) t -> p u e t", u=2, e=2)
-        raw = [keep.tile([P, 2, T], F32, name="raw%d" % u) for u in range(2)]
-        pairs = [keep.tile([P, 2 * T], BF16, name="pairs%d" % u, align_bytes=64) for u in range(2)]
-        picked = keep.tile([P, 2, S], U32, name="picked")
+        x_rows = xT.rearrange("(p j) t -> p j t", j=4)
+        row2 = keep.tile([P, T], F32, name="row2", tag="row2", align_bytes=64)
+        rows01 = keep.tile([P, 2, T], F32, name="rows01")
+        row3 = keep.tile([P, T], F32, name="row3")
+        pairs = keep.tile([P, 2 * T], BF16, name="pairs", align_bytes=64)
 
-        t0 = 0
-        for width, on_vector in LOADS[0]:
-            nc.sync.dma_start(raw[0][:, :, t0 : t0 + width], x_rows[:, 0, :, t0 : t0 + width])
-            t0 = t0 + width
+        nc.sync.dma_start(row2[:], x_rows[:, 2, :])
         nc.sync.dma_start(offs_sb[:], offs)
-        nc.sync.dma_start(raw[1][:, :, :SPLIT], x_rows[:, 1, :, :SPLIT])
-        nc.sync.dma_start(raw[1][:, 0, SPLIT:], x_rows[:, 1, 0, SPLIT:])
-        t0 = SPLIT
-        for width, on_vector in LOADS[1][1:]:
-            nc.sync.dma_start(raw[1][:, 1, t0 : t0 + width], x_rows[:, 1, 1, t0 : t0 + width])
+        t0 = PAIR_LOADS[0][0]
+        nc.sync.dma_start(rows01[:, :, :t0], x_rows[:, 0:2, :t0])
+        nc.sync.dma_start(rows01[:, 0, t0:], x_rows[:, 0, t0:])
+        for width, on_vector in PAIR_LOADS[1:]:
+            nc.sync.dma_start(rows01[:, 1, t0 : t0 + width], x_rows[:, 1, t0 : t0 + width])
+            t0 = t0 + width
+        t0 = 0
+        for width in ROW3_LOADS:
+            nc.sync.dma_start(row3[:, t0 : t0 + width], x_rows[:, 3, t0 : t0 + width])
             t0 = t0 + width
         for q in range(4):
             nc.sync.dma_start(
@@ -67,36 +68,54 @@ def tile_picked_lerp_none_e_kernel(
         nc.sync.dma_start(left_sb[:], left)
         nc.sync.dma_start(frac_sb[:], frac)
 
-        def round_pairs(u):
-            t0 = 0
-            for width, on_vector in LOADS[u]:
-                woven = pairs[u][:, 2 * t0 : 2 * (t0 + width)].rearrange("p (t e) -> p t e", e=2)
-                source = raw[u][:, :, t0 : t0 + width].rearrange("p e t -> p t e")
-                nc.vector.tensor_copy(woven[:, :on_vector, :], source[:, :on_vector, :])
-                if on_vector < width:
-                    nc.scalar.copy(woven[:, on_vector:, :], source[:, on_vector:, :])
-                t0 = t0 + width
+        pieces = S // PIECE
+        entries = [offs_sb[:, i * PIECE // 16 : (i + 1) * PIECE // 16] for i in range(pieces)]
+        picked = keep.tile([P, pieces, 2, PIECE, 2], BF16, name="picked", align_bytes=64)
+        words = picked[:].rearrange("p i u c e -> p i u (c e)")
 
-        round_pairs(0)
-        nc.vector.tensor_copy(picked[:, 0, :], pairs[0][:].bitcast(U32).indirect(offs_sb[:]))
-        round_pairs(1)
+        nc.vector.tensor_copy(picked[:, :, 1, :, 0], row2[:].indirect(offs_sb[:]))
+
+        t0 = 0
+        for width, on_vector in PAIR_LOADS:
+            woven = pairs[:, 2 * t0 : 2 * (t0 + width)].rearrange("p (t e) -> p t e", e=2)
+            source = rows01[:, :, t0 : t0 + width].rearrange("p e t -> p t e")
+            nc.vector.tensor_copy(woven[:, :on_vector, :], source[:, :on_vector, :])
+            nc.scalar.copy(woven[:, on_vector:, :], source[:, on_vector:, :])
+            t0 = t0 + width
+        nc.vector.tensor_copy(words[:, :, 0, :].bitcast(U32), pairs[:].bitcast(U32).indirect(offs_sb[:]))
+
+        row3_bf = keep.tile([P, T], BF16, name="row3_bf", tag="row2", align_bytes=64)
+        t0 = 0
+        for width in ROW3_LOADS:
+            nc.scalar.copy(row3_bf[:, t0 : t0 + width], row3[:, t0 : t0 + width])
+            t0 = t0 + width
+        for i in range(ON_VECTOR):
+            nc.vector.tensor_copy(picked[:, i, 1, :, 1], row3[:].indirect(entries[i]))
+        for i in range(ON_VECTOR, pieces):
+            nc.scalar.activation(picked[:, i, 1, :, 1], row3_bf[:].indirect(entries[i]), COPY)
 
         y = keep.tile([P, S], F32, name="y")
-        pieces = S // PIECE
-        for i in range(pieces):
-            cols = slice(i * PIECE, (i + 1) * PIECE)
-            entries = offs_sb[:, i * PIECE // 16 : (i + 1) * PIECE // 16]
-            nc.vector.tensor_copy(picked[:, 1, cols], pairs[1][:].bitcast(U32).indirect(entries))
-        for i in range(pieces):
-            cols = slice(i * PIECE, (i + 1) * PIECE)
-            grouped = keep.tile([P, 4 * PIECE], BF16, name="grouped%d" % i, tag="grouped%d" % i, align_bytes=64)
-            nc.scalar.copy(
-                grouped[:].bitcast(U32).rearrange("p (c u) -> p c u", u=2),
-                picked[:, :, cols].rearrange("p u c -> p c u"),
-            )
+        grouped = [
+            keep.tile([P, 4 * PIECE], BF16, name="grouped%d" % i, tag="grouped%d" % i, align_bytes=64)
+            for i in range(pieces)
+        ]
+
+        def weave(i):
+            if i >= ON_VECTOR:
+                nc.scalar.copy(
+                    grouped[i][:].bitcast(U32).rearrange("p (c u) -> p c u", u=2),
+                    words[:, i].bitcast(U32).rearrange("p u c -> p c u"),
+                )
+            else:
+                nc.vector.tensor_copy(
+                    grouped[i][:].bitcast(I32).rearrange("p (c u) -> p c u", u=2),
+                    words[:, i].bitcast(I32).rearrange("p u c -> p c u"),
+                )
+
+        def project(i):
             codes = keep.tile([P, PIECE], U32, name="codes%d" % i, align_bytes=64)
             scales = keep.tile([P, PIECE], U8, name="scales%d" % i, align_bytes=64)
-            nc.vector.quantize_mx(out=codes[:].bitcast(FP8X4), scales=scales[:], in_=grouped[:])
+            nc.vector.quantize_mx(out=codes[:].bitcast(FP8X4), scales=scales[:], in_=grouped[i][:])
             parts = 2 if i == pieces - 1 else 1
             width = PIECE // parts
             for h in range(parts):
@@ -113,19 +132,25 @@ def tile_picked_lerp_none_e_kernel(
                 )
                 y_part = y[:, i * PIECE + h * width : i * PIECE + (h + 1) * width]
                 if h + 1 < parts:
-                    rest = keep.tile([P, V], F32, name="rest", tag="grouped%d" % i, align_bytes=64)
                     nc.vector.tensor_scalar(rest[:], frac_sb[:], -1.0, 1.0, MULT, ADD)
                     nc.vector.tensor_copy(y_part, acc[:])
                 else:
                     nc.scalar.copy(y_part, acc[:])
+
+        for i in range(pieces):
+            weave(i)
+        for i in range(pieces - 1):
+            project(i)
+        rest = keep.tile([P, V], F32, name="rest", tag="grouped%d" % (pieces - 1), align_bytes=64)
+        project(pieces - 1)
 
         from_right = keep.tile([P, V], F32, name="from_right")
         from_left = keep.tile([P, V], F32, name="from_left")
         nc.vector.tensor_tensor(from_right[:], y[:].indirect(right_sb[:]), frac_sb[:], MULT)
         halves = [slice(0, V // 2), slice(V // 2, V)]
         for cols in halves:
-            entries = left_sb[:, cols.start // 16 : cols.stop // 16]
-            nc.vector.tensor_tensor(from_left[:, cols], y[:].indirect(entries), rest[:, cols], MULT)
+            part = left_sb[:, cols.start // 16 : cols.stop // 16]
+            nc.vector.tensor_tensor(from_left[:, cols], y[:].indirect(part), rest[:, cols], MULT)
         for cols in halves:
             result = keep.tile([P, V // 2], F32, name="result%d" % cols.start)
             nc.vector.tensor_tensor(result[:], from_right[:, cols], from_left[:, cols], ADD)

@@ -18,10 +18,15 @@ MULT = mybir.AluOpType.mult
 ADD = mybir.AluOpType.add
 COPY = mybir.ActivationFunctionType.Copy
 
-PAIR_LOADS = ((1024, 384), (512, 336), (256, 176), (256, 176))
-ROW3_LOADS = (512, 512, 512, 512)
-ON_VECTOR = 2
+LOADS = (
+    ((2048, None),),
+    ((1024, 0), (1024, 688)),
+    ((2048, None),),
+    ((512, 0), (512, 0), (512, 0), (256, 0), (256, 256)),
+)
 PIECE = 256
+PIECES = S // PIECE
+ON_VECTOR = 2
 
 
 def tile_picked_lerp_none_e_kernel(
@@ -41,23 +46,15 @@ def tile_picked_lerp_none_e_kernel(
         nc.vector.memset(w_scales[:].bitcast(I32), 0)
 
         x_rows = xT.rearrange("(p j) t -> p j t", j=4)
-        row2 = keep.tile([P, T], F32, name="row2", tag="row2", align_bytes=64)
-        rows01 = keep.tile([P, 2, T], F32, name="rows01")
-        row3 = keep.tile([P, T], F32, name="row3")
-        pairs = keep.tile([P, 2 * T], BF16, name="pairs", align_bytes=64)
-
-        nc.sync.dma_start(row2[:], x_rows[:, 2, :])
-        nc.sync.dma_start(offs_sb[:], offs)
-        t0 = PAIR_LOADS[0][0]
-        nc.sync.dma_start(rows01[:, :, :t0], x_rows[:, 0:2, :t0])
-        nc.sync.dma_start(rows01[:, 0, t0:], x_rows[:, 0, t0:])
-        for width, on_vector in PAIR_LOADS[1:]:
-            nc.sync.dma_start(rows01[:, 1, t0 : t0 + width], x_rows[:, 1, t0 : t0 + width])
-            t0 = t0 + width
-        t0 = 0
-        for width in ROW3_LOADS:
-            nc.sync.dma_start(row3[:, t0 : t0 + width], x_rows[:, 3, t0 : t0 + width])
-            t0 = t0 + width
+        exact = [keep.tile([P, T], F32, name="exact%d" % j, align_bytes=64) for j in range(4)]
+        rounded = {j: keep.tile([P, T], BF16, name="rounded%d" % j, align_bytes=64) for j in (1, 3)}
+        for j in range(4):
+            t0 = 0
+            for width, on_vector in LOADS[j]:
+                nc.sync.dma_start(exact[j][:, t0 : t0 + width], x_rows[:, j, t0 : t0 + width])
+                t0 = t0 + width
+            if j == 0:
+                nc.sync.dma_start(offs_sb[:], offs)
         for q in range(4):
             nc.sync.dma_start(
                 w_scales[32 * q : 32 * q + 4, :].bitcast(I32),
@@ -68,36 +65,39 @@ def tile_picked_lerp_none_e_kernel(
         nc.sync.dma_start(left_sb[:], left)
         nc.sync.dma_start(frac_sb[:], frac)
 
-        pieces = S // PIECE
-        entries = [offs_sb[:, i * PIECE // 16 : (i + 1) * PIECE // 16] for i in range(pieces)]
-        picked = keep.tile([P, pieces, 2, PIECE, 2], BF16, name="picked", align_bytes=64)
+        picked = keep.tile([P, PIECES, 2, PIECE, 2], BF16, name="picked", align_bytes=64)
         words = picked[:].rearrange("p i u c e -> p i u (c e)")
 
-        nc.vector.tensor_copy(picked[:, :, 1, :, 0], row2[:].indirect(offs_sb[:]))
+        def entries(first, last):
+            return offs_sb[:, first * PIECE // 16 : last * PIECE // 16]
 
-        t0 = 0
-        for width, on_vector in PAIR_LOADS:
-            woven = pairs[:, 2 * t0 : 2 * (t0 + width)].rearrange("p (t e) -> p t e", e=2)
-            source = rows01[:, :, t0 : t0 + width].rearrange("p e t -> p t e")
-            nc.vector.tensor_copy(woven[:, :on_vector, :], source[:, :on_vector, :])
-            nc.scalar.copy(woven[:, on_vector:, :], source[:, on_vector:, :])
-            t0 = t0 + width
-        nc.vector.tensor_copy(words[:, :, 0, :].bitcast(U32), pairs[:].bitcast(U32).indirect(offs_sb[:]))
-
-        row3_bf = keep.tile([P, T], BF16, name="row3_bf", tag="row2", align_bytes=64)
-        t0 = 0
-        for width in ROW3_LOADS:
-            nc.scalar.copy(row3_bf[:, t0 : t0 + width], row3[:, t0 : t0 + width])
-            t0 = t0 + width
-        for i in range(ON_VECTOR):
-            nc.vector.tensor_copy(picked[:, i, 1, :, 1], row3[:].indirect(entries[i]))
-        for i in range(ON_VECTOR, pieces):
-            nc.scalar.activation(picked[:, i, 1, :, 1], row3_bf[:].indirect(entries[i]), COPY)
+        for j in range(4):
+            t0 = 0
+            if j % 2 == 0:
+                nc.vector.tensor_copy(picked[:, :, j // 2, :, 0], exact[j][:].indirect(offs_sb[:]))
+                continue
+            for width, on_vector in LOADS[j]:
+                t1 = t0 + on_vector
+                if on_vector > 0:
+                    nc.vector.tensor_copy(rounded[j][:, t0:t1], exact[j][:, t0:t1])
+                if on_vector < width:
+                    nc.scalar.copy(rounded[j][:, t1 : t0 + width], exact[j][:, t1 : t0 + width])
+                t0 = t0 + width
+            step = 1 if j == 3 else ON_VECTOR
+            for i in range(0, ON_VECTOR, step):
+                nc.vector.tensor_copy(
+                    picked[:, i : i + step, j // 2, :, j % 2], exact[j][:].indirect(entries(i, i + step))
+                )
+            step = 1 if j == 3 else PIECES - ON_VECTOR
+            for i in range(ON_VECTOR, PIECES, step):
+                nc.scalar.activation(
+                    picked[:, i : i + step, j // 2, :, j % 2], rounded[j][:].indirect(entries(i, i + step)), COPY
+                )
 
         y = keep.tile([P, S], F32, name="y")
         grouped = [
             keep.tile([P, 4 * PIECE], BF16, name="grouped%d" % i, tag="grouped%d" % i, align_bytes=64)
-            for i in range(pieces)
+            for i in range(PIECES)
         ]
 
         def weave(i):
@@ -116,7 +116,7 @@ def tile_picked_lerp_none_e_kernel(
             codes = keep.tile([P, PIECE], U32, name="codes%d" % i, align_bytes=64)
             scales = keep.tile([P, PIECE], U8, name="scales%d" % i, align_bytes=64)
             nc.vector.quantize_mx(out=codes[:].bitcast(FP8X4), scales=scales[:], in_=grouped[i][:])
-            parts = 2 if i == pieces - 1 else 1
+            parts = 2 if i == PIECES - 1 else 1
             width = PIECE // parts
             for h in range(parts):
                 part = slice(h * width, (h + 1) * width)
@@ -137,12 +137,12 @@ def tile_picked_lerp_none_e_kernel(
                 else:
                     nc.scalar.copy(y_part, acc[:])
 
-        for i in range(pieces):
+        for i in range(PIECES):
             weave(i)
-        for i in range(pieces - 1):
+        for i in range(PIECES - 1):
             project(i)
-        rest = keep.tile([P, V], F32, name="rest", tag="grouped%d" % (pieces - 1), align_bytes=64)
-        project(pieces - 1)
+        rest = keep.tile([P, V], F32, name="rest", tag="grouped%d" % (PIECES - 1), align_bytes=64)
+        project(PIECES - 1)
 
         from_right = keep.tile([P, V], F32, name="from_right")
         from_left = keep.tile([P, V], F32, name="from_left")

@@ -20,13 +20,14 @@ COPY = mybir.ActivationFunctionType.Copy
 
 LOADS = (
     ((2048, None),),
-    ((1024, 0), (1024, 688)),
+    ((2048, 1376),),
     ((2048, None),),
     ((512, 0), (512, 0), (512, 0), (256, 0), (256, 256)),
 )
 PIECE = 256
 PIECES = S // PIECE
 ON_VECTOR = 2
+SHARE = 128
 
 
 def tile_picked_lerp_none_e_kernel(
@@ -100,24 +101,30 @@ def tile_picked_lerp_none_e_kernel(
             for i in range(PIECES)
         ]
 
-        def weave(i):
-            if i >= ON_VECTOR:
-                nc.scalar.copy(
-                    grouped[i][:].bitcast(U32).rearrange("p (c u) -> p c u", u=2),
-                    words[:, i].bitcast(U32).rearrange("p u c -> p c u"),
-                )
-            else:
-                nc.vector.tensor_copy(
-                    grouped[i][:].bitcast(I32).rearrange("p (c u) -> p c u", u=2),
-                    words[:, i].bitcast(I32).rearrange("p u c -> p c u"),
-                )
+        def weave_scalar(i, cols):
+            nc.scalar.copy(
+                grouped[i][:].bitcast(U32).rearrange("p (c u) -> p c u", u=2)[:, cols, :],
+                words[:, i].bitcast(U32).rearrange("p u c -> p c u")[:, cols, :],
+            )
+
+        def weave_vector(i, cols):
+            nc.vector.tensor_copy(
+                grouped[i][:].bitcast(I32).rearrange("p (c u) -> p c u", u=2)[:, cols, :],
+                words[:, i].bitcast(I32).rearrange("p u c -> p c u")[:, cols, :],
+            )
 
         def project(i):
             codes = keep.tile([P, PIECE], U32, name="codes%d" % i, align_bytes=64)
             scales = keep.tile([P, PIECE], U8, name="scales%d" % i, align_bytes=64)
-            nc.vector.quantize_mx(out=codes[:].bitcast(FP8X4), scales=scales[:], in_=grouped[i][:])
             parts = 2 if i == PIECES - 1 else 1
             width = PIECE // parts
+            for h in range(parts):
+                part = slice(h * width, (h + 1) * width)
+                nc.vector.quantize_mx(
+                    out=codes[:, part].bitcast(FP8X4),
+                    scales=scales[:, part],
+                    in_=grouped[i][:, 4 * part.start : 4 * part.stop],
+                )
             for h in range(parts):
                 part = slice(h * width, (h + 1) * width)
                 acc = psum.tile([P, width], F32, name="acc%d_%d" % (i, h))
@@ -137,10 +144,15 @@ def tile_picked_lerp_none_e_kernel(
                 else:
                     nc.scalar.copy(y_part, acc[:])
 
-        for i in range(PIECES):
-            weave(i)
-        for i in range(PIECES - 1):
-            project(i)
+        whole = slice(0, PIECE)
+        weave_vector(0, whole)
+        weave_vector(1, whole)
+        weave_scalar(2, whole)
+        weave_scalar(3, slice(0, SHARE))
+        project(0)
+        project(1)
+        project(2)
+        weave_vector(3, slice(SHARE, PIECE))
         rest = keep.tile([P, V], F32, name="rest", tag="grouped%d" % (PIECES - 1), align_bytes=64)
         project(PIECES - 1)
 

@@ -27,7 +27,6 @@ LOADS = (
 PIECE = 256
 PIECES = S // PIECE
 ON_VECTOR = 2
-SHARE = 128
 
 
 def tile_picked_lerp_none_e_kernel(
@@ -148,22 +147,30 @@ def tile_picked_lerp_none_e_kernel(
         weave_vector(0, whole)
         weave_vector(1, whole)
         weave_scalar(2, whole)
-        weave_scalar(3, slice(0, SHARE))
+        weave_scalar(3, whole)
         project(0)
         project(1)
         project(2)
-        weave_vector(3, slice(SHARE, PIECE))
         rest = keep.tile([P, V], F32, name="rest", tag="grouped%d" % (PIECES - 1), align_bytes=64)
         project(PIECES - 1)
 
         from_right = keep.tile([P, V], F32, name="from_right")
         from_left = keep.tile([P, V], F32, name="from_left")
         nc.vector.tensor_tensor(from_right[:], y[:].indirect(right_sb[:]), frac_sb[:], MULT)
-        halves = [slice(0, V // 2), slice(V // 2, V)]
-        for cols in halves:
+        parts = [slice(0, 256), slice(256, 384), slice(384, 512)]
+
+        def fetch_left(cols):
             part = left_sb[:, cols.start // 16 : cols.stop // 16]
             nc.vector.tensor_tensor(from_left[:, cols], y[:].indirect(part), rest[:, cols], MULT)
-        for cols in halves:
-            result = keep.tile([P, V // 2], F32, name="result%d" % cols.start)
+
+        def finish(cols):
+            result = keep.tile([P, cols.stop - cols.start], F32, name="result%d" % cols.start)
             nc.vector.tensor_tensor(result[:], from_right[:, cols], from_left[:, cols], ADD)
             nc.sync.dma_start(out[:, cols], result[:])
+
+        fetch_left(parts[0])
+        fetch_left(parts[1])
+        finish(parts[0])
+        fetch_left(parts[2])
+        finish(parts[1])
+        finish(parts[2])

@@ -22,7 +22,7 @@ LOADS = (
     ((2048, None),),
     ((2048, 1376),),
     ((2048, None),),
-    ((512, 0), (512, 0), (512, 0), (256, 0), (256, 256)),
+    ((2048, None),),
 )
 PIECE = 256
 PIECES = S // PIECE
@@ -47,7 +47,7 @@ def tile_picked_lerp_none_e_kernel(
 
         x_rows = xT.rearrange("(p j) t -> p j t", j=4)
         exact = [keep.tile([P, T], F32, name="exact%d" % j, align_bytes=64) for j in range(4)]
-        rounded = {j: keep.tile([P, T], BF16, name="rounded%d" % j, align_bytes=64) for j in (1, 3)}
+        rounded = {j: keep.tile([P, T], BF16, name="rounded%d" % j, align_bytes=64) for j in (1,)}
         for j in range(4):
             t0 = 0
             for width, on_vector in LOADS[j]:
@@ -75,6 +75,10 @@ def tile_picked_lerp_none_e_kernel(
             t0 = 0
             if j % 2 == 0:
                 nc.vector.tensor_copy(picked[:, :, j // 2, :, 0], exact[j][:].indirect(offs_sb[:]))
+                continue
+            if j == 3:
+                for i in range(PIECES):
+                    nc.vector.tensor_copy(picked[:, i, 1, :, 1], exact[j][:].indirect(entries(i, i + 1)))
                 continue
             for width, on_vector in LOADS[j]:
                 t1 = t0 + on_vector
@@ -144,8 +148,8 @@ def tile_picked_lerp_none_e_kernel(
                     nc.scalar.copy(y_part, acc[:])
 
         whole = slice(0, PIECE)
-        weave_vector(0, whole)
-        weave_vector(1, whole)
+        weave_scalar(0, whole)
+        weave_scalar(1, whole)
         weave_scalar(2, whole)
         weave_scalar(3, whole)
         project(0)

@@ -18,15 +18,12 @@ MULT = mybir.AluOpType.mult
 ADD = mybir.AluOpType.add
 COPY = mybir.ActivationFunctionType.Copy
 
-LOADS = (
-    ((2048, None),),
-    ((2048, 1376),),
-    ((2048, None),),
-    ((2048, None),),
-)
+ROW_ORDER = (0, 2, 1, 3)
 PIECE = 256
 PIECES = S // PIECE
-ON_VECTOR = 2
+HALF = PIECES // 2
+ROUNDED_BY_VECTOR = 1152
+OUT_PARTS = (slice(0, V // 2), slice(V // 2, 3 * V // 4), slice(3 * V // 4, V))
 
 
 def tile_picked_lerp_none_e_kernel(
@@ -47,13 +44,10 @@ def tile_picked_lerp_none_e_kernel(
 
         x_rows = xT.rearrange("(p j) t -> p j t", j=4)
         exact = [keep.tile([P, T], F32, name="exact%d" % j, align_bytes=64) for j in range(4)]
-        rounded = {j: keep.tile([P, T], BF16, name="rounded%d" % j, align_bytes=64) for j in (1,)}
-        for j in range(4):
-            t0 = 0
-            for width, on_vector in LOADS[j]:
-                nc.sync.dma_start(exact[j][:, t0 : t0 + width], x_rows[:, j, t0 : t0 + width])
-                t0 = t0 + width
-            if j == 0:
+        rounded1 = keep.tile([P, T], BF16, name="rounded1", align_bytes=64)
+        for j in ROW_ORDER:
+            nc.sync.dma_start(exact[j][:], x_rows[:, j, :])
+            if j == ROW_ORDER[0]:
                 nc.sync.dma_start(offs_sb[:], offs)
         for q in range(4):
             nc.sync.dma_start(
@@ -65,103 +59,75 @@ def tile_picked_lerp_none_e_kernel(
         nc.sync.dma_start(left_sb[:], left)
         nc.sync.dma_start(frac_sb[:], frac)
 
-        picked = keep.tile([P, PIECES, 2, PIECE, 2], BF16, name="picked", align_bytes=64)
-        words = picked[:].rearrange("p i u c e -> p i u (c e)")
+        picked = keep.tile([P, PIECES, 2, PIECE, 2], BF16, name="picked", tag="picked", align_bytes=64)
+        pairs = picked[:].rearrange("p i u c e -> p i u (c e)")
 
         def entries(first, last):
             return offs_sb[:, first * PIECE // 16 : last * PIECE // 16]
 
-        for j in range(4):
-            t0 = 0
-            if j % 2 == 0:
-                nc.vector.tensor_copy(picked[:, :, j // 2, :, 0], exact[j][:].indirect(offs_sb[:]))
-                continue
-            if j == 3:
-                for i in range(PIECES):
-                    nc.vector.tensor_copy(picked[:, i, 1, :, 1], exact[j][:].indirect(entries(i, i + 1)))
-                continue
-            for width, on_vector in LOADS[j]:
-                t1 = t0 + on_vector
-                if on_vector > 0:
-                    nc.vector.tensor_copy(rounded[j][:, t0:t1], exact[j][:, t0:t1])
-                if on_vector < width:
-                    nc.scalar.copy(rounded[j][:, t1 : t0 + width], exact[j][:, t1 : t0 + width])
-                t0 = t0 + width
-            step = 1 if j == 3 else ON_VECTOR
-            for i in range(0, ON_VECTOR, step):
-                nc.vector.tensor_copy(
-                    picked[:, i : i + step, j // 2, :, j % 2], exact[j][:].indirect(entries(i, i + step))
-                )
-            step = 1 if j == 3 else PIECES - ON_VECTOR
-            for i in range(ON_VECTOR, PIECES, step):
-                nc.scalar.activation(
-                    picked[:, i : i + step, j // 2, :, j % 2], rounded[j][:].indirect(entries(i, i + step)), COPY
-                )
+        def slots(j, first, last):
+            return picked[:, first:last, j // 2, :, j % 2]
 
-        y = keep.tile([P, S], F32, name="y")
+        for j in (0, 2):
+            nc.vector.tensor_copy(slots(j, 0, PIECES), exact[j][:].indirect(offs_sb[:]))
+
+        nc.vector.tensor_copy(rounded1[:, :ROUNDED_BY_VECTOR], exact[1][:, :ROUNDED_BY_VECTOR])
+        nc.scalar.copy(rounded1[:, ROUNDED_BY_VECTOR:], exact[1][:, ROUNDED_BY_VECTOR:])
+        nc.vector.tensor_copy(slots(1, 0, HALF), exact[1][:].indirect(entries(0, HALF)))
+        nc.scalar.activation(slots(1, HALF, PIECES), rounded1[:].indirect(entries(HALF, PIECES)), COPY)
+
+        y = keep.tile([P, S], F32, name="y", tag="picked", align_bytes=64)
         grouped = [
             keep.tile([P, 4 * PIECE], BF16, name="grouped%d" % i, tag="grouped%d" % i, align_bytes=64)
             for i in range(PIECES)
         ]
+        codes = [keep.tile([P, PIECE], U32, name="codes%d" % i, align_bytes=64) for i in range(PIECES)]
+        scales = [keep.tile([P, PIECE], U8, name="scales%d" % i, align_bytes=64) for i in range(PIECES)]
 
-        def weave_scalar(i, cols):
+        def weave(i, cols):
             nc.scalar.copy(
                 grouped[i][:].bitcast(U32).rearrange("p (c u) -> p c u", u=2)[:, cols, :],
-                words[:, i].bitcast(U32).rearrange("p u c -> p c u")[:, cols, :],
+                pairs[:, i].bitcast(U32).rearrange("p u c -> p c u")[:, cols, :],
             )
 
-        def weave_vector(i, cols):
-            nc.vector.tensor_copy(
-                grouped[i][:].bitcast(I32).rearrange("p (c u) -> p c u", u=2)[:, cols, :],
-                words[:, i].bitcast(I32).rearrange("p u c -> p c u")[:, cols, :],
+        def project(i, cols):
+            nc.vector.quantize_mx(
+                out=codes[i][:, cols].bitcast(FP8X4),
+                scales=scales[i][:, cols],
+                in_=grouped[i][:, 4 * cols.start : 4 * cols.stop],
             )
+            acc = psum.tile([P, cols.stop - cols.start], F32, name="acc%d_%d" % (i, cols.start))
+            nc.tensor.matmul_mx(
+                out=acc[:],
+                lhsT=w_codes[:].bitcast(FP4X4),
+                lhsT_scale=w_scales[:],
+                rhs=codes[i][:, cols].bitcast(FP8X4),
+                rhs_scale=scales[i][:, cols],
+                start=True,
+                stop=True,
+            )
+            return y[:, i * PIECE + cols.start : i * PIECE + cols.stop], acc[:]
 
-        def project(i):
-            codes = keep.tile([P, PIECE], U32, name="codes%d" % i, align_bytes=64)
-            scales = keep.tile([P, PIECE], U8, name="scales%d" % i, align_bytes=64)
-            parts = 2 if i == PIECES - 1 else 1
-            width = PIECE // parts
-            for h in range(parts):
-                part = slice(h * width, (h + 1) * width)
-                nc.vector.quantize_mx(
-                    out=codes[:, part].bitcast(FP8X4),
-                    scales=scales[:, part],
-                    in_=grouped[i][:, 4 * part.start : 4 * part.stop],
-                )
-            for h in range(parts):
-                part = slice(h * width, (h + 1) * width)
-                acc = psum.tile([P, width], F32, name="acc%d_%d" % (i, h))
-                nc.tensor.matmul_mx(
-                    out=acc[:],
-                    lhsT=w_codes[:].bitcast(FP4X4),
-                    lhsT_scale=w_scales[:],
-                    rhs=codes[:, part].bitcast(FP8X4),
-                    rhs_scale=scales[:, part],
-                    start=True,
-                    stop=True,
-                )
-                y_part = y[:, i * PIECE + h * width : i * PIECE + (h + 1) * width]
-                if h + 1 < parts:
-                    nc.vector.tensor_scalar(rest[:], frac_sb[:], -1.0, 1.0, MULT, ADD)
-                    nc.vector.tensor_copy(y_part, acc[:])
-                else:
-                    nc.scalar.copy(y_part, acc[:])
-
-        whole = slice(0, PIECE)
-        weave_scalar(0, whole)
-        weave_scalar(1, whole)
-        weave_scalar(2, whole)
-        weave_scalar(3, whole)
-        project(0)
-        project(1)
-        project(2)
-        rest = keep.tile([P, V], F32, name="rest", tag="grouped%d" % (PIECES - 1), align_bytes=64)
-        project(PIECES - 1)
+        last = PIECES - 1
+        whole, lower, upper = slice(0, PIECE), slice(0, PIECE // 2), slice(PIECE // 2, PIECE)
+        for i in range(PIECES):
+            nc.vector.tensor_copy(picked[:, i, 1, :, 1], exact[3][:].indirect(entries(i, i + 1)))
+        for i in range(last):
+            weave(i, whole)
+        weave(last, lower)
+        weave(last, upper)
+        for i in range(last):
+            nc.scalar.copy(*project(i, whole))
+        last_lower = project(last, lower)
+        last_upper = project(last, upper)
+        rest = keep.tile([P, V], F32, name="rest", tag="grouped%d" % last, align_bytes=64)
+        nc.vector.tensor_scalar(rest[:], frac_sb[:], -1.0, 1.0, MULT, ADD)
+        nc.vector.tensor_copy(*last_lower)
+        nc.scalar.copy(*last_upper)
 
         from_right = keep.tile([P, V], F32, name="from_right")
         from_left = keep.tile([P, V], F32, name="from_left")
         nc.vector.tensor_tensor(from_right[:], y[:].indirect(right_sb[:]), frac_sb[:], MULT)
-        parts = [slice(0, 256), slice(256, 384), slice(384, 512)]
 
         def fetch_left(cols):
             part = left_sb[:, cols.start // 16 : cols.stop // 16]
@@ -172,9 +138,8 @@ def tile_picked_lerp_none_e_kernel(
             nc.vector.tensor_tensor(result[:], from_right[:, cols], from_left[:, cols], ADD)
             nc.sync.dma_start(out[:, cols], result[:])
 
-        fetch_left(parts[0])
-        fetch_left(parts[1])
-        finish(parts[0])
-        fetch_left(parts[2])
-        finish(parts[1])
-        finish(parts[2])
+        fetch_left(OUT_PARTS[0])
+        for n in range(1, len(OUT_PARTS)):
+            fetch_left(OUT_PARTS[n])
+            finish(OUT_PARTS[n - 1])
+        finish(OUT_PARTS[-1])

@@ -18,11 +18,9 @@ MULT = mybir.AluOpType.mult
 ADD = mybir.AluOpType.add
 COPY = mybir.ActivationFunctionType.Copy
 
-ROW_ORDER = (0, 2, 1, 3)
 PIECE = 256
 PIECES = S // PIECE
-HALF = PIECES // 2
-ROUNDED_BY_VECTOR = 1152
+PAIRED = 2
 OUT_PARTS = (slice(0, V // 2), slice(V // 2, 3 * V // 4), slice(3 * V // 4, V))
 
 
@@ -44,10 +42,9 @@ def tile_picked_lerp_none_e_kernel(
 
         x_rows = xT.rearrange("(p j) t -> p j t", j=4)
         exact = [keep.tile([P, T], F32, name="exact%d" % j, align_bytes=64) for j in range(4)]
-        rounded1 = keep.tile([P, T], BF16, name="rounded1", align_bytes=64)
-        for j in ROW_ORDER:
+        for j in range(4):
             nc.sync.dma_start(exact[j][:], x_rows[:, j, :])
-            if j == ROW_ORDER[0]:
+            if j == 0:
                 nc.sync.dma_start(offs_sb[:], offs)
         for q in range(4):
             nc.sync.dma_start(
@@ -59,30 +56,30 @@ def tile_picked_lerp_none_e_kernel(
         nc.sync.dma_start(left_sb[:], left)
         nc.sync.dma_start(frac_sb[:], frac)
 
-        picked = keep.tile([P, PIECES, 2, PIECE, 2], BF16, name="picked", tag="picked", align_bytes=64)
-        pairs = picked[:].rearrange("p i u c e -> p i u (c e)")
-
         def entries(first, last):
             return offs_sb[:, first * PIECE // 16 : last * PIECE // 16]
 
-        def slots(j, first, last):
-            return picked[:, first:last, j // 2, :, j % 2]
-
-        for j in (0, 2):
-            nc.vector.tensor_copy(slots(j, 0, PIECES), exact[j][:].indirect(offs_sb[:]))
-
-        nc.vector.tensor_copy(rounded1[:, :ROUNDED_BY_VECTOR], exact[1][:, :ROUNDED_BY_VECTOR])
-        nc.scalar.copy(rounded1[:, ROUNDED_BY_VECTOR:], exact[1][:, ROUNDED_BY_VECTOR:])
-        nc.vector.tensor_copy(slots(1, 0, HALF), exact[1][:].indirect(entries(0, HALF)))
-        nc.scalar.activation(slots(1, HALF, PIECES), rounded1[:].indirect(entries(HALF, PIECES)), COPY)
-
-        y = keep.tile([P, S], F32, name="y", tag="picked", align_bytes=64)
+        picked = keep.tile([P, PAIRED, 2, PIECE, 2], BF16, name="picked", align_bytes=64)
+        pairs = picked[:].rearrange("p i u c e -> p i u (c e)")
+        y = keep.tile([P, S], F32, name="y", align_bytes=64)
         grouped = [
             keep.tile([P, 4 * PIECE], BF16, name="grouped%d" % i, tag="grouped%d" % i, align_bytes=64)
             for i in range(PIECES)
         ]
         codes = [keep.tile([P, PIECE], U32, name="codes%d" % i, align_bytes=64) for i in range(PIECES)]
         scales = [keep.tile([P, PIECE], U8, name="scales%d" % i, align_bytes=64) for i in range(PIECES)]
+        dense = {}
+        for i in range(PAIRED, PIECES):
+            dense[i] = keep.tile([P, 4 * PIECE], BF16, name="dense%d" % i, align_bytes=64)
+
+        def fetch(j, i):
+            nc.scalar.activation(dense[i][:, j * PIECE : (j + 1) * PIECE], exact[j][:].indirect(entries(i, i + 1)), COPY)
+
+        def place(first, last, i, cols):
+            nc.vector.tensor_copy(
+                grouped[i][:].rearrange("p (c j) -> p c j", j=4)[:, cols, first:last],
+                dense[i][:].rearrange("p (j c) -> p c j", j=4)[:, cols, first:last],
+            )
 
         def weave(i, cols):
             nc.scalar.copy(
@@ -90,15 +87,27 @@ def tile_picked_lerp_none_e_kernel(
                 pairs[:, i].bitcast(U32).rearrange("p u c -> p c u")[:, cols, :],
             )
 
-        def project(i, cols):
+        whole, lower, upper = slice(0, PIECE), slice(0, PIECE // 2), slice(PIECE // 2, PIECE)
+        for j in range(4):
+            for i in range(PAIRED, PIECES):
+                fetch(j, i)
+            if j < 3:
+                nc.vector.tensor_copy(picked[:, :, j // 2, :, j % 2], exact[j][:].indirect(entries(0, PAIRED)))
+            else:
+                for i in range(PAIRED):
+                    nc.vector.tensor_copy(picked[:, i, 1, :, 1], exact[j][:].indirect(entries(i, i + 1)))
+            if j == 1:
+                for i in range(PAIRED, PIECES):
+                    place(0, 2, i, whole)
+
+        def project(i, cols, acc):
             nc.vector.quantize_mx(
                 out=codes[i][:, cols].bitcast(FP8X4),
                 scales=scales[i][:, cols],
                 in_=grouped[i][:, 4 * cols.start : 4 * cols.stop],
             )
-            acc = psum.tile([P, cols.stop - cols.start], F32, name="acc%d_%d" % (i, cols.start))
             nc.tensor.matmul_mx(
-                out=acc[:],
+                out=acc,
                 lhsT=w_codes[:].bitcast(FP4X4),
                 lhsT_scale=w_scales[:],
                 rhs=codes[i][:, cols].bitcast(FP8X4),
@@ -106,40 +115,40 @@ def tile_picked_lerp_none_e_kernel(
                 start=True,
                 stop=True,
             )
-            return y[:, i * PIECE + cols.start : i * PIECE + cols.stop], acc[:]
 
-        last = PIECES - 1
-        whole, lower, upper = slice(0, PIECE), slice(0, PIECE // 2), slice(PIECE // 2, PIECE)
-        for i in range(PIECES):
-            nc.vector.tensor_copy(picked[:, i, 1, :, 1], exact[3][:].indirect(entries(i, i + 1)))
-        for i in range(last):
+        last = PAIRED - 1
+        banks = [psum.tile([P, PIECE], F32, name="acc%d" % i) for i in range(PIECES)]
+        spare = psum.tile([P, PIECE // 2], F32, name="spare")
+        for i in range(PAIRED):
             weave(i, whole)
-        weave(last, lower)
-        weave(last, upper)
-        for i in range(last):
-            nc.scalar.copy(*project(i, whole))
-        last_lower = project(last, lower)
-        last_upper = project(last, upper)
+        place(2, 4, 2, whole)
+        place(2, 4, 3, lower)
+        project(2, whole, banks[2][:])
+        place(2, 4, 3, upper)
+        for i in (3, 0):
+            project(i, lower, banks[i][:, lower])
+            project(i, upper, banks[i][:, upper])
+        project(last, lower, banks[last][:, lower])
+        project(last, upper, spare[:])
+        for i in (2, 3, 0):
+            nc.scalar.copy(y[:, i * PIECE : (i + 1) * PIECE], banks[i][:])
+        last_lower = (y[:, last * PIECE : last * PIECE + PIECE // 2], banks[last][:, lower])
+        last_upper = (y[:, last * PIECE + PIECE // 2 : (last + 1) * PIECE], spare[:])
         rest = keep.tile([P, V], F32, name="rest", tag="grouped%d" % last, align_bytes=64)
         nc.vector.tensor_scalar(rest[:], frac_sb[:], -1.0, 1.0, MULT, ADD)
         nc.vector.tensor_copy(*last_lower)
         nc.scalar.copy(*last_upper)
 
         from_right = keep.tile([P, V], F32, name="from_right")
+        at_left = keep.tile([P, V], F32, name="at_left")
         from_left = keep.tile([P, V], F32, name="from_left")
+        halves = (slice(0, V // 2), slice(V // 2, V))
+        for cols in halves:
+            nc.scalar.activation(at_left[:, cols], y[:].indirect(left_sb[:, cols.start // 16 : cols.stop // 16]), COPY)
         nc.vector.tensor_tensor(from_right[:], y[:].indirect(right_sb[:]), frac_sb[:], MULT)
-
-        def fetch_left(cols):
-            part = left_sb[:, cols.start // 16 : cols.stop // 16]
-            nc.vector.tensor_tensor(from_left[:, cols], y[:].indirect(part), rest[:, cols], MULT)
-
-        def finish(cols):
+        for cols in halves:
+            nc.vector.tensor_tensor(from_left[:, cols], at_left[:, cols], rest[:, cols], MULT)
+        for cols in OUT_PARTS:
             result = keep.tile([P, cols.stop - cols.start], F32, name="result%d" % cols.start)
             nc.vector.tensor_tensor(result[:], from_right[:, cols], from_left[:, cols], ADD)
             nc.sync.dma_start(out[:, cols], result[:])
-
-        fetch_left(OUT_PARTS[0])
-        for n in range(1, len(OUT_PARTS)):
-            fetch_left(OUT_PARTS[n])
-            finish(OUT_PARTS[n - 1])
-        finish(OUT_PARTS[-1])

@@ -16,6 +16,7 @@ FP8X4 = mybir.dt.float8_e4m3fn_x4
 FP4X4 = mybir.dt.float4_e2m1fn_x4
 MULT = mybir.AluOpType.mult
 ADD = mybir.AluOpType.add
+SUBTRACT = mybir.AluOpType.subtract
 COPY = mybir.ActivationFunctionType.Copy
 
 PIECE = 256
@@ -68,18 +69,26 @@ def tile_picked_lerp_none_e_kernel(
         ]
         codes = [keep.tile([P, PIECE], U32, name="codes%d" % i, align_bytes=64) for i in range(PIECES)]
         scales = [keep.tile([P, PIECE], U8, name="scales%d" % i, align_bytes=64) for i in range(PIECES)]
-        dense = {}
-        for i in range(PAIRED, PIECES):
-            dense[i] = keep.tile([P, 4 * PIECE], BF16, name="dense%d" % i, align_bytes=64)
+        placed = (PIECES - PAIRED) * PIECE
+        dense = keep.tile([P, 4 * placed], BF16, name="dense", align_bytes=64)
+        dense_rows = dense[:].rearrange("p (j c) -> p c j", j=4)
 
-        def fetch(j, i):
-            nc.scalar.activation(dense[i][:, j * PIECE : (j + 1) * PIECE], exact[j][:].indirect(entries(i, i + 1)), COPY)
+        def fetch(j, start, stop):
+            part = offs_sb[:, (PAIRED * PIECE + start) // 16 : (PAIRED * PIECE + stop) // 16]
+            nc.scalar.activation(dense[:, j * placed + start : j * placed + stop], exact[j][:].indirect(part), COPY)
+
+        def sides(first, last, i, cols):
+            start = (i - PAIRED) * PIECE
+            return (
+                grouped[i][:].rearrange("p (c j) -> p c j", j=4)[:, cols, first:last],
+                dense_rows[:, start + cols.start : start + cols.stop, first:last],
+            )
 
         def place(first, last, i, cols):
-            nc.vector.tensor_copy(
-                grouped[i][:].rearrange("p (c j) -> p c j", j=4)[:, cols, first:last],
-                dense[i][:].rearrange("p (j c) -> p c j", j=4)[:, cols, first:last],
-            )
+            nc.vector.tensor_copy(*sides(first, last, i, cols))
+
+        def place_aside(first, last, i, cols):
+            nc.gpsimd.tensor_scalar(*sides(first, last, i, cols), 1.0, 0.0, MULT, ADD)
 
         def weave(i, cols):
             nc.scalar.copy(
@@ -89,16 +98,14 @@ def tile_picked_lerp_none_e_kernel(
 
         whole, lower, upper = slice(0, PIECE), slice(0, PIECE // 2), slice(PIECE // 2, PIECE)
         for j in range(4):
-            for i in range(PAIRED, PIECES):
-                fetch(j, i)
-            if j < 3:
-                nc.vector.tensor_copy(picked[:, :, j // 2, :, j % 2], exact[j][:].indirect(entries(0, PAIRED)))
-            else:
-                for i in range(PAIRED):
-                    nc.vector.tensor_copy(picked[:, i, 1, :, 1], exact[j][:].indirect(entries(i, i + 1)))
+            fetch(j, 0, PIECE // 2)
+            fetch(j, PIECE // 2, 3 * PIECE // 2)
+            fetch(j, 3 * PIECE // 2, placed)
+            nc.vector.tensor_copy(picked[:, :, j // 2, :, j % 2], exact[j][:].indirect(entries(0, PAIRED)))
             if j == 1:
-                for i in range(PAIRED, PIECES):
-                    place(0, 2, i, whole)
+                place_aside(0, 2, 2, lower)
+                place(0, 2, 2, upper)
+                place(0, 2, 3, whole)
 
         def project(i, cols, acc):
             nc.vector.quantize_mx(
@@ -121,9 +128,11 @@ def tile_picked_lerp_none_e_kernel(
         spare = psum.tile([P, PIECE // 2], F32, name="spare")
         for i in range(PAIRED):
             weave(i, whole)
-        place(2, 4, 2, whole)
+        place_aside(2, 4, 2, lower)
+        project(2, lower, banks[2][:, lower])
+        place(2, 4, 2, upper)
         place(2, 4, 3, lower)
-        project(2, whole, banks[2][:])
+        project(2, upper, banks[2][:, upper])
         place(2, 4, 3, upper)
         for i in (3, 0):
             project(i, lower, banks[i][:, lower])
@@ -134,8 +143,6 @@ def tile_picked_lerp_none_e_kernel(
             nc.scalar.copy(y[:, i * PIECE : (i + 1) * PIECE], banks[i][:])
         last_lower = (y[:, last * PIECE : last * PIECE + PIECE // 2], banks[last][:, lower])
         last_upper = (y[:, last * PIECE + PIECE // 2 : (last + 1) * PIECE], spare[:])
-        rest = keep.tile([P, V], F32, name="rest", tag="grouped%d" % last, align_bytes=64)
-        nc.vector.tensor_scalar(rest[:], frac_sb[:], -1.0, 1.0, MULT, ADD)
         nc.vector.tensor_copy(*last_lower)
         nc.scalar.copy(*last_upper)
 
@@ -147,8 +154,8 @@ def tile_picked_lerp_none_e_kernel(
             nc.scalar.activation(at_left[:, cols], y[:].indirect(left_sb[:, cols.start // 16 : cols.stop // 16]), COPY)
         nc.vector.tensor_tensor(from_right[:], y[:].indirect(right_sb[:]), frac_sb[:], MULT)
         for cols in halves:
-            nc.vector.tensor_tensor(from_left[:, cols], at_left[:, cols], rest[:, cols], MULT)
+            nc.vector.scalar_tensor_tensor(from_left[:, cols], frac_sb[:, cols], 1.0, at_left[:, cols], SUBTRACT, MULT)
         for cols in OUT_PARTS:
             result = keep.tile([P, cols.stop - cols.start], F32, name="result%d" % cols.start)
-            nc.vector.tensor_tensor(result[:], from_right[:, cols], from_left[:, cols], ADD)
+            nc.vector.tensor_tensor(result[:], from_right[:, cols], from_left[:, cols], SUBTRACT)
             nc.sync.dma_start(out[:, cols], result[:])

@@ -21,7 +21,7 @@ COPY = mybir.ActivationFunctionType.Copy
 
 PIECE = 256
 PIECES = S // PIECE
-PAIRED = 2
+PAIRED = 3
 OUT_PARTS = (slice(0, V // 2), slice(V // 2, 3 * V // 4), slice(3 * V // 4, V))
 
 
@@ -84,9 +84,6 @@ def tile_picked_lerp_none_e_kernel(
                 dense_rows[:, start + cols.start : start + cols.stop, first:last],
             )
 
-        def place(first, last, i, cols):
-            nc.vector.tensor_copy(*sides(first, last, i, cols))
-
         def place_aside(first, last, i, cols):
             nc.gpsimd.tensor_scalar(*sides(first, last, i, cols), 1.0, 0.0, MULT, ADD)
 
@@ -97,15 +94,15 @@ def tile_picked_lerp_none_e_kernel(
             )
 
         whole, lower, upper = slice(0, PIECE), slice(0, PIECE // 2), slice(PIECE // 2, PIECE)
-        for j in range(4):
-            fetch(j, 0, PIECE // 2)
-            fetch(j, PIECE // 2, 3 * PIECE // 2)
-            fetch(j, 3 * PIECE // 2, placed)
+        for j in range(3):
+            fetch(j, 0, PIECE)
             nc.vector.tensor_copy(picked[:, :, j // 2, :, j % 2], exact[j][:].indirect(entries(0, PAIRED)))
             if j == 1:
-                place_aside(0, 2, 2, lower)
-                place(0, 2, 2, upper)
-                place(0, 2, 3, whole)
+                place_aside(0, 2, 3, whole)
+        fetch(3, 0, PIECE // 2)
+        fetch(3, PIECE // 2, PIECE)
+        for i in range(PAIRED):
+            nc.vector.tensor_copy(picked[:, i, 1, :, 1], exact[3][:].indirect(entries(i, i + 1)))
 
         def project(i, cols, acc):
             nc.vector.quantize_mx(
@@ -126,20 +123,18 @@ def tile_picked_lerp_none_e_kernel(
         last = PAIRED - 1
         banks = [psum.tile([P, PIECE], F32, name="acc%d" % i) for i in range(PIECES)]
         spare = psum.tile([P, PIECE // 2], F32, name="spare")
-        for i in range(PAIRED):
+        for i in range(last):
             weave(i, whole)
-        place_aside(2, 4, 2, lower)
-        project(2, lower, banks[2][:, lower])
-        place(2, 4, 2, upper)
-        place(2, 4, 3, lower)
-        project(2, upper, banks[2][:, upper])
-        place(2, 4, 3, upper)
-        for i in (3, 0):
+        weave(last, lower)
+        weave(last, upper)
+        place_aside(2, 4, 3, lower)
+        place_aside(2, 4, 3, upper)
+        for i in (3, 0, 1):
             project(i, lower, banks[i][:, lower])
             project(i, upper, banks[i][:, upper])
         project(last, lower, banks[last][:, lower])
         project(last, upper, spare[:])
-        for i in (2, 3, 0):
+        for i in (3, 0, 1):
             nc.scalar.copy(y[:, i * PIECE : (i + 1) * PIECE], banks[i][:])
         last_lower = (y[:, last * PIECE : last * PIECE + PIECE // 2], banks[last][:, lower])
         last_upper = (y[:, last * PIECE + PIECE // 2 : (last + 1) * PIECE], spare[:])

@@ -22,7 +22,8 @@ COPY = mybir.ActivationFunctionType.Copy
 PIECE = 256
 PIECES = S // PIECE
 PAIRED = 3
-OUT_PARTS = (slice(0, V // 2), slice(V // 2, 3 * V // 4), slice(3 * V // 4, V))
+EARLY_BY_VECTOR = 480
+OUT_PARTS = (slice(0, 256), slice(256, 384), slice(384, 512))
 
 
 def tile_picked_lerp_none_e_kernel(
@@ -41,12 +42,17 @@ def tile_picked_lerp_none_e_kernel(
         frac_sb = keep.tile([P, V], F32, name="frac_sb")
         nc.vector.memset(w_scales[:].bitcast(I32), 0)
 
+        idle = keep.tile([P, 2], F32, name="idle")
+        nc.vector.memset(idle[:, 0:1], 0.0)
+        nc.scalar.activation(idle[:, 1:2], idle[:, 0:1], COPY)
+
         x_rows = xT.rearrange("(p j) t -> p j t", j=4)
-        exact = [keep.tile([P, T], F32, name="exact%d" % j, align_bytes=64) for j in range(4)]
-        for j in range(4):
+        early = keep.tile([P, 2 * T], F32, name="early", align_bytes=64)
+        nc.sync.dma_start(early[:], x_rows[:, 0:2, :].rearrange("p j t -> p (j t)"))
+        nc.sync.dma_start(offs_sb[:], offs)
+        exact = {j: keep.tile([P, T], F32, name="exact%d" % j, align_bytes=64) for j in (2, 3)}
+        for j in exact:
             nc.sync.dma_start(exact[j][:], x_rows[:, j, :])
-            if j == 0:
-                nc.sync.dma_start(offs_sb[:], offs)
         for q in range(4):
             nc.sync.dma_start(
                 w_scales[32 * q : 32 * q + 4, :].bitcast(I32),
@@ -60,8 +66,8 @@ def tile_picked_lerp_none_e_kernel(
         def entries(first, last):
             return offs_sb[:, first * PIECE // 16 : last * PIECE // 16]
 
-        picked = keep.tile([P, PAIRED, 2, PIECE, 2], BF16, name="picked", align_bytes=64)
-        pairs = picked[:].rearrange("p i u c e -> p i u (c e)")
+        picked = keep.tile([P, 2, PAIRED * PIECE, 2], BF16, name="picked", align_bytes=64)
+        pairs = picked[:].rearrange("p u c e -> p u (c e)").bitcast(U32).rearrange("p u c -> p c u")
         y = keep.tile([P, S], F32, name="y", align_bytes=64)
         grouped = [
             keep.tile([P, 4 * PIECE], BF16, name="grouped%d" % i, tag="grouped%d" % i, align_bytes=64)
@@ -90,19 +96,27 @@ def tile_picked_lerp_none_e_kernel(
         def weave(i, cols):
             nc.scalar.copy(
                 grouped[i][:].bitcast(U32).rearrange("p (c u) -> p c u", u=2)[:, cols, :],
-                pairs[:, i].bitcast(U32).rearrange("p u c -> p c u")[:, cols, :],
+                pairs[:, i * PIECE + cols.start : i * PIECE + cols.stop, :],
             )
 
         whole, lower, upper = slice(0, PIECE), slice(0, PIECE // 2), slice(PIECE // 2, PIECE)
-        for j in range(3):
-            fetch(j, 0, PIECE)
-            nc.vector.tensor_copy(picked[:, :, j // 2, :, j % 2], exact[j][:].indirect(entries(0, PAIRED)))
-            if j == 1:
-                place_aside(0, 2, 3, whole)
+        rest = S - EARLY_BY_VECTOR
+        wide = keep.tile([P, 2 * rest], F32, name="wide", align_bytes=64)
+        wide_rows = wide[:].rearrange("p (j c) -> p c j", j=2)
+        for j in range(2):
+            row = early[:, j * T : (j + 1) * T]
+            nc.scalar.activation(wide[:, j * rest : (j + 1) * rest], row.indirect(offs_sb[:, EARLY_BY_VECTOR // 16 :]), COPY)
+            nc.vector.tensor_copy(picked[:, 0, :EARLY_BY_VECTOR, j], row.indirect(offs_sb[:, : EARLY_BY_VECTOR // 16]))
+        nc.gpsimd.tensor_scalar(
+            grouped[3][:].rearrange("p (c j) -> p c j", j=4)[:, :, 0:2], wide_rows[:, rest - PIECE :, :], 1.0, 0.0, MULT, ADD
+        )
+        nc.scalar.copy(picked[:, 0, EARLY_BY_VECTOR:, :], wide_rows[:, : rest - PIECE, :])
+        fetch(2, 0, PIECE)
+        nc.vector.tensor_copy(picked[:, 1, :, 0], exact[2][:].indirect(entries(0, PAIRED)))
         fetch(3, 0, PIECE // 2)
         fetch(3, PIECE // 2, PIECE)
         for i in range(PAIRED):
-            nc.vector.tensor_copy(picked[:, i, 1, :, 1], exact[3][:].indirect(entries(i, i + 1)))
+            nc.vector.tensor_copy(picked[:, 1, i * PIECE : (i + 1) * PIECE, 1], exact[3][:].indirect(entries(i, i + 1)))
 
         def project(i, cols, acc):
             nc.vector.quantize_mx(
@@ -148,9 +162,17 @@ def tile_picked_lerp_none_e_kernel(
         for cols in halves:
             nc.scalar.activation(at_left[:, cols], y[:].indirect(left_sb[:, cols.start // 16 : cols.stop // 16]), COPY)
         nc.vector.tensor_tensor(from_right[:], y[:].indirect(right_sb[:]), frac_sb[:], MULT)
-        for cols in halves:
+
+        def weigh_left(cols):
             nc.vector.scalar_tensor_tensor(from_left[:, cols], frac_sb[:, cols], 1.0, at_left[:, cols], SUBTRACT, MULT)
-        for cols in OUT_PARTS:
+
+        def finish(cols):
             result = keep.tile([P, cols.stop - cols.start], F32, name="result%d" % cols.start)
             nc.vector.tensor_tensor(result[:], from_right[:, cols], from_left[:, cols], SUBTRACT)
             nc.sync.dma_start(out[:, cols], result[:])
+
+        weigh_left(OUT_PARTS[0])
+        for n in range(1, len(OUT_PARTS)):
+            weigh_left(OUT_PARTS[n])
+            finish(OUT_PARTS[n - 1])
+        finish(OUT_PARTS[-1])

@@ -23,7 +23,7 @@ PIECE = 256
 PIECES = S // PIECE
 PAIRED = 3
 EARLY_BY_VECTOR = 480
-OUT_PARTS = (slice(0, 256), slice(256, 384), slice(384, 512))
+OUT_PARTS = tuple(slice(n * V // 4, (n + 1) * V // 4) for n in range(4))
 
 
 def tile_picked_lerp_none_e_kernel(
@@ -171,8 +171,10 @@ def tile_picked_lerp_none_e_kernel(
             nc.vector.tensor_tensor(result[:], from_right[:, cols], from_left[:, cols], SUBTRACT)
             nc.sync.dma_start(out[:, cols], result[:])
 
-        weigh_left(OUT_PARTS[0])
-        for n in range(1, len(OUT_PARTS)):
-            weigh_left(OUT_PARTS[n])
-            finish(OUT_PARTS[n - 1])
-        finish(OUT_PARTS[-1])
+        for cols in OUT_PARTS[:3]:
+            weigh_left(cols)
+        for cols in OUT_PARTS[:2]:
+            finish(cols)
+        weigh_left(OUT_PARTS[3])
+        for cols in OUT_PARTS[2:]:
+            finish(cols)

@@ -158,10 +158,15 @@ def tile_picked_lerp_none_e_kernel(
         from_right = keep.tile([P, V], F32, name="from_right")
         at_left = keep.tile([P, V], F32, name="at_left")
         from_left = keep.tile([P, V], F32, name="from_left")
-        halves = (slice(0, V // 2), slice(V // 2, V))
-        for cols in halves:
+        at_right = keep.tile([P, V // 4], F32, name="at_right")
+        final = OUT_PARTS[3]
+        cut = final.start // 2
+        for cols in (slice(0, cut), slice(cut, final.start), final):
             nc.scalar.activation(at_left[:, cols], y[:].indirect(left_sb[:, cols.start // 16 : cols.stop // 16]), COPY)
-        nc.vector.tensor_tensor(from_right[:], y[:].indirect(right_sb[:]), frac_sb[:], MULT)
+        nc.scalar.activation(at_right[:], y[:].indirect(right_sb[:, final.start // 16 :]), COPY)
+        nc.vector.tensor_tensor(
+            from_right[:, : final.start], y[:].indirect(right_sb[:, : final.start // 16]), frac_sb[:, : final.start], MULT
+        )
 
         def weigh_left(cols):
             nc.vector.scalar_tensor_tensor(from_left[:, cols], frac_sb[:, cols], 1.0, at_left[:, cols], SUBTRACT, MULT)
@@ -175,6 +180,7 @@ def tile_picked_lerp_none_e_kernel(
             weigh_left(cols)
         for cols in OUT_PARTS[:2]:
             finish(cols)
-        weigh_left(OUT_PARTS[3])
+        weigh_left(final)
+        nc.vector.tensor_tensor(from_right[:, final], at_right[:], frac_sb[:, final], MULT)
         for cols in OUT_PARTS[2:]:
             finish(cols)

@@ -23,6 +23,7 @@ PIECE = 256
 PIECES = S // PIECE
 PAIRED = 3
 EARLY_BY_VECTOR = 480
+RIGHT_BY_VECTOR = 416
 OUT_PARTS = tuple(slice(n * V // 4, (n + 1) * V // 4) for n in range(4))
 
 
@@ -158,15 +159,13 @@ def tile_picked_lerp_none_e_kernel(
         from_right = keep.tile([P, V], F32, name="from_right")
         at_left = keep.tile([P, V], F32, name="at_left")
         from_left = keep.tile([P, V], F32, name="from_left")
-        at_right = keep.tile([P, V // 4], F32, name="at_right")
         final = OUT_PARTS[3]
-        cut = final.start // 2
-        for cols in (slice(0, cut), slice(cut, final.start), final):
+        mine, theirs = slice(0, RIGHT_BY_VECTOR), slice(RIGHT_BY_VECTOR, V)
+        at_right = keep.tile([P, V - RIGHT_BY_VECTOR], F32, name="at_right")
+        for cols in (slice(0, V // 2), OUT_PARTS[2], final):
             nc.scalar.activation(at_left[:, cols], y[:].indirect(left_sb[:, cols.start // 16 : cols.stop // 16]), COPY)
-        nc.scalar.activation(at_right[:], y[:].indirect(right_sb[:, final.start // 16 :]), COPY)
-        nc.vector.tensor_tensor(
-            from_right[:, : final.start], y[:].indirect(right_sb[:, : final.start // 16]), frac_sb[:, : final.start], MULT
-        )
+        nc.scalar.activation(at_right[:], y[:].indirect(right_sb[:, theirs.start // 16 :]), COPY)
+        nc.vector.tensor_tensor(from_right[:, mine], y[:].indirect(right_sb[:, : mine.stop // 16]), frac_sb[:, mine], MULT)
 
         def weigh_left(cols):
             nc.vector.scalar_tensor_tensor(from_left[:, cols], frac_sb[:, cols], 1.0, at_left[:, cols], SUBTRACT, MULT)
@@ -181,6 +180,6 @@ def tile_picked_lerp_none_e_kernel(
         for cols in OUT_PARTS[:2]:
             finish(cols)
         weigh_left(final)
-        nc.vector.tensor_tensor(from_right[:, final], at_right[:], frac_sb[:, final], MULT)
+        nc.vector.tensor_tensor(from_right[:, theirs], at_right[:], frac_sb[:, theirs], MULT)
         for cols in OUT_PARTS[2:]:
             finish(cols)

@@ -38,8 +38,8 @@ def tile_picked_lerp_none_e_kernel(
         offs_sb = keep.tile([P, S // 16], U16, name="offs_sb")
         left_sb = keep.tile([P, V // 16], U16, name="left_sb")
         right_sb = keep.tile([P, V // 16], U16, name="right_sb")
-        w_codes = keep.tile([P, 2 * N], U8, name="w_codes", align_bytes=64)
-        w_scales = keep.tile([P, N], U8, name="w_scales", align_bytes=64)
+        w_codes = keep.tile([P, 2 * N], U8, name="w_codes", align_bytes=256)
+        w_scales = keep.tile([P, N], U8, name="w_scales", align_bytes=256)
         frac_sb = keep.tile([P, V], F32, name="frac_sb")
         nc.vector.memset(w_scales[:].bitcast(I32), 0)
 
@@ -74,8 +74,8 @@ def tile_picked_lerp_none_e_kernel(
             keep.tile([P, 4 * PIECE], BF16, name="grouped%d" % i, tag="grouped%d" % i, align_bytes=64)
             for i in range(PIECES)
         ]
-        codes = [keep.tile([P, PIECE], U32, name="codes%d" % i, align_bytes=64) for i in range(PIECES)]
-        scales = [keep.tile([P, PIECE], U8, name="scales%d" % i, align_bytes=64) for i in range(PIECES)]
+        codes = [keep.tile([P, PIECE], U32, name="codes%d" % i, align_bytes=256) for i in range(PIECES)]
+        scales = [keep.tile([P, PIECE], U8, name="scales%d" % i, align_bytes=256) for i in range(PIECES)]
         placed = (PIECES - PAIRED) * PIECE
         dense = keep.tile([P, 4 * placed], BF16, name="dense", align_bytes=64)
         dense_rows = dense[:].rearrange("p (j c) -> p c j", j=4)

@@ -77,7 +77,7 @@ def tile_picked_lerp_none_e_kernel(
         codes = [keep.tile([P, PIECE], U32, name="codes%d" % i, align_bytes=256) for i in range(PIECES)]
         scales = [keep.tile([P, PIECE], U8, name="scales%d" % i, align_bytes=256) for i in range(PIECES)]
         placed = (PIECES - PAIRED) * PIECE
-        dense = keep.tile([P, 4 * placed], BF16, name="dense", align_bytes=64)
+        dense = keep.tile([P, 4 * placed], F32, name="dense", align_bytes=64)
         dense_rows = dense[:].rearrange("p (j c) -> p c j", j=4)
 
         def fetch(j, start, stop):

@@ -106,12 +106,14 @@ def tile_picked_lerp_none_e_kernel(
         wide_rows = wide[:].rearrange("p (j c) -> p c j", j=2)
         for j in range(2):
             row = early[:, j * T : (j + 1) * T]
-            nc.scalar.activation(wide[:, j * rest : (j + 1) * rest], row.indirect(offs_sb[:, EARLY_BY_VECTOR // 16 :]), COPY)
+            for start, stop in ((0, rest),) if j == 0 else ((0, rest - PIECE), (rest - PIECE, rest)):
+                part = offs_sb[:, (EARLY_BY_VECTOR + start) // 16 : (EARLY_BY_VECTOR + stop) // 16]
+                nc.scalar.activation(wide[:, j * rest + start : j * rest + stop], row.indirect(part), COPY)
             nc.vector.tensor_copy(picked[:, 0, :EARLY_BY_VECTOR, j], row.indirect(offs_sb[:, : EARLY_BY_VECTOR // 16]))
+        nc.gpsimd.tensor_scalar(picked[:, 0, EARLY_BY_VECTOR:, :], wide_rows[:, : rest - PIECE, :], 1.0, 0.0, MULT, ADD)
         nc.gpsimd.tensor_scalar(
             grouped[3][:].rearrange("p (c j) -> p c j", j=4)[:, :, 0:2], wide_rows[:, rest - PIECE :, :], 1.0, 0.0, MULT, ADD
         )
-        nc.scalar.copy(picked[:, 0, EARLY_BY_VECTOR:, :], wide_rows[:, : rest - PIECE, :])
         fetch(2, 0, PIECE)
         nc.vector.tensor_copy(picked[:, 1, :, 0], exact[2][:].indirect(entries(0, PAIRED)))
         fetch(3, 0, PIECE // 2)

@@ -146,17 +146,21 @@ def tile_picked_lerp_none_e_kernel(
         weave(last, upper)
         place_aside(2, 4, 3, lower)
         place_aside(2, 4, 3, upper)
-        for i in (3, 0, 1):
+        aside = psum.tile([P, PIECE // 2], F32, name="aside")
+        for i in (3, 0):
             project(i, lower, banks[i][:, lower])
             project(i, upper, banks[i][:, upper])
+        project(1, lower, banks[1][:, lower])
+        project(1, upper, aside[:])
         project(last, lower, banks[last][:, lower])
         project(last, upper, spare[:])
-        for i in (3, 0, 1):
+        half = PIECE // 2
+        for i in (3, 0):
             nc.scalar.copy(y[:, i * PIECE : (i + 1) * PIECE], banks[i][:])
-        last_lower = (y[:, last * PIECE : last * PIECE + PIECE // 2], banks[last][:, lower])
-        last_upper = (y[:, last * PIECE + PIECE // 2 : (last + 1) * PIECE], spare[:])
-        nc.vector.tensor_copy(*last_lower)
-        nc.scalar.copy(*last_upper)
+        nc.scalar.copy(y[:, PIECE : PIECE + half], banks[1][:, lower])
+        nc.vector.tensor_copy(y[:, PIECE + half : last * PIECE], aside[:])
+        nc.scalar.copy(y[:, last * PIECE : last * PIECE + half], banks[last][:, lower])
+        nc.scalar.copy(y[:, last * PIECE + half : (last + 1) * PIECE], spare[:])
 
         from_right = keep.tile([P, V], F32, name="from_right")
         at_left = keep.tile([P, V], F32, name="at_left")

from contextlib import ExitStack

import concourse.mybir as mybir

K, T, S, V, N = 512, 2048, 1024, 512, 128
P = 128
FLOPS = 2 * K * N * S

F32 = mybir.dt.float32
BF16 = mybir.dt.bfloat16
I32 = mybir.dt.int32
U32 = mybir.dt.uint32
U16 = mybir.dt.uint16
U8 = mybir.dt.uint8
FP8X4 = mybir.dt.float8_e4m3fn_x4
FP4X4 = mybir.dt.float4_e2m1fn_x4
MULT = mybir.AluOpType.mult
ADD = mybir.AluOpType.add
SUBTRACT = mybir.AluOpType.subtract
COPY = mybir.ActivationFunctionType.Copy

PIECE = 256
PIECES = S // PIECE
PAIRED = 3
EARLY_BY_VECTOR = 480
RIGHT_BY_VECTOR = 416
OUT_PARTS = tuple(slice(n * V // 4, (n + 1) * V // 4) for n in range(4))


def tile_picked_lerp_none_e_kernel(
    tc, xT, w1_words, w1_scales, frac, offs, left, right, out
):
    nc = tc.nc
    with ExitStack() as ctx:
        keep = ctx.enter_context(tc.tile_pool(name="keep", bufs=1))
        psum = ctx.enter_context(tc.psum_pool(name="psum", bufs=1))

        offs_sb = keep.tile([P, S // 16], U16, name="offs_sb")
        left_sb = keep.tile([P, V // 16], U16, name="left_sb")
        right_sb = keep.tile([P, V // 16], U16, name="right_sb")
        w_codes = keep.tile([P, 2 * N], U8, name="w_codes", align_bytes=256)
        w_scales = keep.tile([P, N], U8, name="w_scales", align_bytes=256)
        frac_sb = keep.tile([P, V], F32, name="frac_sb")
        nc.vector.memset(w_scales[:].bitcast(I32), 0)

        idle = keep.tile([P, 2], F32, name="idle")
        nc.vector.memset(idle[:, 0:1], 0.0)
        nc.scalar.activation(idle[:, 1:2], idle[:, 0:1], COPY)

        x_rows = xT.rearrange("(p j) t -> p j t", j=4)
        early = keep.tile([P, 2 * T], F32, name="early", align_bytes=64)
        nc.sync.dma_start(early[:], x_rows[:, 0:2, :].rearrange("p j t -> p (j t)"))
        nc.sync.dma_start(offs_sb[:], offs)
        exact = {j: keep.tile([P, T], F32, name="exact%d" % j, align_bytes=64) for j in (2, 3)}
        for j in exact:
            nc.sync.dma_start(exact[j][:], x_rows[:, j, :])
        for q in range(4):
            nc.sync.dma_start(
                w_scales[32 * q : 32 * q + 4, :].bitcast(I32),
                w1_scales[0, 4 * q : 4 * q + 4, :].bitcast(I32),
            )
        nc.sync.dma_start(w_codes[:].bitcast(I32), w1_words[0].bitcast(I32))
        nc.sync.dma_start(right_sb[:], right)
        nc.sync.dma_start(left_sb[:], left)
        nc.sync.dma_start(frac_sb[:], frac)

        def entries(first, last):
            return offs_sb[:, first * PIECE // 16 : last * PIECE // 16]

        picked = keep.tile([P, 2, PAIRED * PIECE, 2], BF16, name="picked", align_bytes=64)
        pairs = picked[:].rearrange("p u c e -> p u (c e)").bitcast(U32).rearrange("p u c -> p c u")
        y = keep.tile([P, S], F32, name="y", align_bytes=64)
        grouped = [
            keep.tile([P, 4 * PIECE], BF16, name="grouped%d" % i, tag="grouped%d" % i, align_bytes=64)
            for i in range(PIECES)
        ]
        codes = [keep.tile([P, PIECE], U32, name="codes%d" % i, align_bytes=256) for i in range(PIECES)]
        scales = [keep.tile([P, PIECE], U8, name="scales%d" % i, align_bytes=256) for i in range(PIECES)]
        placed = (PIECES - PAIRED) * PIECE
        dense = keep.tile([P, 4 * placed], F32, name="dense", align_bytes=64)
        dense_rows = dense[:].rearrange("p (j c) -> p c j", j=4)

        def fetch(j, start, stop):
            part = offs_sb[:, (PAIRED * PIECE + start) // 16 : (PAIRED * PIECE + stop) // 16]
            nc.scalar.activation(dense[:, j * placed + start : j * placed + stop], exact[j][:].indirect(part), COPY)

        def sides(first, last, i, cols):
            start = (i - PAIRED) * PIECE
            return (
                grouped[i][:].rearrange("p (c j) -> p c j", j=4)[:, cols, first:last],
                dense_rows[:, start + cols.start : start + cols.stop, first:last],
            )

        def place_aside(first, last, i, cols):
            nc.gpsimd.tensor_scalar(*sides(first, last, i, cols), 1.0, 0.0, MULT, ADD)

        def weave(i, cols):
            nc.scalar.copy(
                grouped[i][:].bitcast(U32).rearrange("p (c u) -> p c u", u=2)[:, cols, :],
                pairs[:, i * PIECE + cols.start : i * PIECE + cols.stop, :],
            )

        whole, lower, upper = slice(0, PIECE), slice(0, PIECE // 2), slice(PIECE // 2, PIECE)
        rest = S - EARLY_BY_VECTOR
        wide = keep.tile([P, 2 * rest], F32, name="wide", align_bytes=64)
        wide_rows = wide[:].rearrange("p (j c) -> p c j", j=2)
        for j in range(2):
            row = early[:, j * T : (j + 1) * T]
            for start, stop in ((0, rest),) if j == 0 else ((0, rest - PIECE), (rest - PIECE, rest)):
                part = offs_sb[:, (EARLY_BY_VECTOR + start) // 16 : (EARLY_BY_VECTOR + stop) // 16]
                nc.scalar.activation(wide[:, j * rest + start : j * rest + stop], row.indirect(part), COPY)
            nc.vector.tensor_copy(picked[:, 0, :EARLY_BY_VECTOR, j], row.indirect(offs_sb[:, : EARLY_BY_VECTOR // 16]))
        nc.gpsimd.tensor_scalar(picked[:, 0, EARLY_BY_VECTOR:, :], wide_rows[:, : rest - PIECE, :], 1.0, 0.0, MULT, ADD)
        nc.gpsimd.tensor_scalar(
            grouped[3][:].rearrange("p (c j) -> p c j", j=4)[:, :, 0:2], wide_rows[:, rest - PIECE :, :], 1.0, 0.0, MULT, ADD
        )
        fetch(2, 0, PIECE)
        nc.vector.tensor_copy(picked[:, 1, :, 0], exact[2][:].indirect(entries(0, PAIRED)))
        fetch(3, 0, PIECE // 2)
        fetch(3, PIECE // 2, PIECE)
        for i in range(PAIRED):
            nc.vector.tensor_copy(picked[:, 1, i * PIECE : (i + 1) * PIECE, 1], exact[3][:].indirect(entries(i, i + 1)))

        def project(i, cols, acc):
            nc.vector.quantize_mx(
                out=codes[i][:, cols].bitcast(FP8X4),
                scales=scales[i][:, cols],
                in_=grouped[i][:, 4 * cols.start : 4 * cols.stop],
            )
            nc.tensor.matmul_mx(
                out=acc,
                lhsT=w_codes[:].bitcast(FP4X4),
                lhsT_scale=w_scales[:],
                rhs=codes[i][:, cols].bitcast(FP8X4),
                rhs_scale=scales[i][:, cols],
                start=True,
                stop=True,
            )

        last = PAIRED - 1
        banks = [psum.tile([P, PIECE], F32, name="acc%d" % i) for i in range(PIECES)]
        spare = psum.tile([P, PIECE // 2], F32, name="spare")
        for i in range(last):
            weave(i, whole)
        weave(last, lower)
        weave(last, upper)
        place_aside(2, 4, 3, lower)
        place_aside(2, 4, 3, upper)
        aside = psum.tile([P, PIECE // 2], F32, name="aside")
        for i in (3, 0):
            project(i, lower, banks[i][:, lower])
            project(i, upper, banks[i][:, upper])
        project(1, lower, banks[1][:, lower])
        project(1, upper, aside[:])
        project(last, lower, banks[last][:, lower])
        project(last, upper, spare[:])
        half = PIECE // 2
        for i in (3, 0):
            nc.scalar.copy(y[:, i * PIECE : (i + 1) * PIECE], banks[i][:])
        nc.scalar.copy(y[:, PIECE : PIECE + half], banks[1][:, lower])
        nc.vector.tensor_copy(y[:, PIECE + half : last * PIECE], aside[:])
        nc.scalar.copy(y[:, last * PIECE : last * PIECE + half], banks[last][:, lower])
        nc.scalar.copy(y[:, last * PIECE + half : (last + 1) * PIECE], spare[:])

        from_right = keep.tile([P, V], F32, name="from_right")
        at_left = keep.tile([P, V], F32, name="at_left")
        from_left = keep.tile([P, V], F32, name="from_left")
        final = OUT_PARTS[3]
        mine, theirs = slice(0, RIGHT_BY_VECTOR), slice(RIGHT_BY_VECTOR, V)
        at_right = keep.tile([P, V - RIGHT_BY_VECTOR], F32, name="at_right")
        for cols in (slice(0, V // 2), OUT_PARTS[2], final):
            nc.scalar.activation(at_left[:, cols], y[:].indirect(left_sb[:, cols.start // 16 : cols.stop // 16]), COPY)
        nc.scalar.activation(at_right[:], y[:].indirect(right_sb[:, theirs.start // 16 :]), COPY)
        nc.vector.tensor_tensor(from_right[:, mine], y[:].indirect(right_sb[:, : mine.stop // 16]), frac_sb[:, mine], MULT)

        def weigh_left(cols):
            nc.vector.scalar_tensor_tensor(from_left[:, cols], frac_sb[:, cols], 1.0, at_left[:, cols], SUBTRACT, MULT)

        def finish(cols):
            result = keep.tile([P, cols.stop - cols.start], F32, name="result%d" % cols.start)
            nc.vector.tensor_tensor(result[:], from_right[:, cols], from_left[:, cols], SUBTRACT)
            nc.sync.dma_start(out[:, cols], result[:])

        for cols in OUT_PARTS[:3]:
            weigh_left(cols)
        for cols in OUT_PARTS[:2]:
            finish(cols)
        weigh_left(final)
        nc.vector.tensor_tensor(from_right[:, theirs], at_right[:], frac_sb[:, theirs], MULT)
        for cols in OUT_PARTS[2:]:
            finish(cols)
